import numpy as np
import ml_dtypes


def mxq(x, axis, fmt="e4m3"):
    dtype, down = {"e4m3": (ml_dtypes.float8_e4m3fn, 7), "e5m2": (ml_dtypes.float8_e5m2, 14)}[fmt]
    v = np.moveaxis(np.asarray(x, np.float32).astype(ml_dtypes.bfloat16).astype(np.float64), axis, -1)
    blocks = v.reshape(v.shape[:-1] + (-1, 32))
    amax = np.abs(blocks).max(-1, keepdims=True)
    byte = np.maximum(np.where(amax > 0, np.frexp(amax)[1] - 1 + 127, 0) - down, 1)
    scale = np.exp2(byte - 127.0)
    codes = (blocks / scale).astype(np.float32).astype(dtype).astype(np.float64)
    return np.moveaxis((codes * scale).reshape(v.shape), -1, axis)


WIDE = False


def mx_kscale(k):
    if not WIDE:
        return np.ones(k)
    levels = np.array([10, -10, 5, -5, 0])
    if k % 512:
        return np.exp2(np.random.permutation(np.resize(levels, k // 32))).repeat(32)
    a = np.empty((k // 512, 16))
    for p in range(k // 512):
        a[p, :8] = np.random.permutation(np.resize(levels, 8))
        for g in range(8):
            far = levels[np.abs(levels - a[p, g]) >= 10]
            a[p, g + 8] = far[np.random.randint(len(far))]
    return np.exp2(a.ravel()).repeat(32)


def f64(x):
    return np.asarray(x).astype(np.float64)


def striped(idx):
    return np.tile(idx.reshape(-1, 16).T, (8, 1)).astype(np.uint16)


def unstriped(offs):
    return offs[:16].T.reshape(-1).astype(np.int64)


E2M1 = np.array([0.0, 0.5, 1.0, 1.5, 2.0, 3.0, 4.0, 6.0, -0.0, -0.5, -1.0, -1.5, -2.0, -3.0, -4.0, -6.0])


def pack_weight(w, fmt):
    k, n = w.shape
    w = f64(np.asarray(w, np.float32).astype(ml_dtypes.bfloat16)).reshape(k // 32, 32, n)
    amax = np.abs(w).max(1)
    if fmt == "e4m3":
        byte = np.frexp(amax)[1] - 1 + 127 - 7
    else:
        mant, ex = np.frexp(amax / 6.0)
        byte = np.where(mant > 0.5, ex, ex - 1) + 127
    byte = np.clip(np.where(amax > 0, byte, 1), 1, 254)
    scaled = (w * np.exp2(127.0 - byte)[:, None, :]).reshape(k, n).astype(np.float32)
    by_word = np.ascontiguousarray(scaled.reshape(k // 512, 128, 4, n).transpose(0, 1, 3, 2))
    if fmt == "e4m3":
        words = by_word.astype(ml_dtypes.float8_e4m3fn).view(np.uint8)
    else:
        c = by_word.astype(ml_dtypes.float4_e2m1fn).view(np.uint8) & 0xF
        words = (c[..., 0::2] | (c[..., 1::2] << 4)).reshape(k // 512, 128, 2 * n)
    return np.ascontiguousarray(words), np.ascontiguousarray(byte.astype(np.uint8).reshape(k // 512, 16, n))


def unpack_weight(words, scales, fmt):
    g, _, n = scales.shape
    words = np.ascontiguousarray(words).reshape(g, 128, n, -1)
    if fmt == "e4m3":
        vals = words.view(ml_dtypes.float8_e4m3fn).astype(np.float64)
    else:
        nib = np.empty((g, 128, n, 4), np.uint8)
        nib[..., 0::2] = words & 0xF
        nib[..., 1::2] = words >> 4
        vals = E2M1[nib]
    vals = vals * np.repeat(np.exp2(scales.astype(np.float64) - 127.0), 8, axis=1)[..., None]
    return vals.transpose(0, 1, 3, 2).reshape(g * 512, n)


def gelu(v):
    return 0.5 * v * (1.0 + np.tanh(np.sqrt(2.0 / np.pi) * (v + 0.044715 * v**3)))


K, H, T, S, T3, S2, P = 1024, 512, 4096, 1024, 2048, 1024, 512

def setup_inputs():
    n = np.random.standard_normal
    s = mx_kscale(K)[:, None]
    u = mx_kscale(H)[:, None]
    tab_words, tab_scales = pack_weight(n((K, T)) * s, "e4m3")
    tab2_words, tab2_scales = pack_weight(n((H, T3)) / np.sqrt(H) / u, "e4m3")
    w2_words, w2_scales = pack_weight(0.9 * n((K, H)) / np.sqrt(K) / s * u.T, "e2m1")
    return {
        "tab_words": tab_words, "tab_scales": tab_scales,
        "offs": striped(np.random.permutation(T)[:S]),
        "tab2_words": tab2_words, "tab2_scales": tab2_scales,
        "offs2": striped(np.random.permutation(T3)[:S2]),
        "pos1": striped(np.random.permutation(S)[:P]),
        "pos2": striped(np.random.permutation(S)[:P]),
        "w1": (1.5 * n((K, H)) / np.sqrt(K) / s).astype(np.float32),
        "gain": (np.random.uniform(0.7, 1.7, H) * u[:, 0]).astype(np.float32),
        "w2_words": w2_words, "w2_scales": w2_scales,
        "b2": (0.5 * n(H) * u[:, 0]).astype(np.float32),
        "w3": (n((H, S2)) / np.sqrt(H) / u).astype(np.float32),
        "vec": np.random.uniform(4.0, 8.0, S2).astype(np.float32),
        "shift": (0.5 * n((S2, P))).astype(np.float32),
    }

def reference(tab_words, tab_scales, offs, tab2_words, tab2_scales, offs2, pos1, pos2,
              w1, gain, w2_words, w2_scales, b2, w3, vec, shift):
    v = unpack_weight(tab_words, tab_scales, "e4m3")[:, unstriped(offs)]
    v2 = unpack_weight(tab2_words, tab2_scales, "e4m3")[:, unstriped(offs2)]
    w2 = unpack_weight(w2_words, w2_scales, "e2m1")
    h = f64(gain)[:, None] * np.tanh(mxq(f64(w1), 0, "e4m3").T @ v)
    g = (w2.T @ v) + f64(b2)[:, None]
    hq = mxq(h, 0, "e4m3")
    gq = mxq(g, 0, "e4m3")
    e = v2.T @ hq
    d = np.maximum(v2.T @ gq, mxq(f64(w3), 0, "e4m3").T @ gq)
    top = e.max(axis=1)
    a = np.exp(e[:, unstriped(pos1)] - top[:, None])
    return (f64(vec)[:, None] * a + f64(shift)) * d[:, unstriped(pos2)]

@@ -1,0 +1,315 @@
+from contextlib import ExitStack
+
+import concourse.mybir as mybir
+
+K, H, T, S, T3, S2, NP = 1024, 512, 4096, 1024, 2048, 1024, 512
+FLOPS = 2 * (2 * K * H * S + 3 * H * S2 * S)
+
+F32 = mybir.dt.float32
+BF16 = mybir.dt.bfloat16
+I32 = mybir.dt.int32
+U32 = mybir.dt.uint32
+U16 = mybir.dt.uint16
+U8 = mybir.dt.uint8
+FP8X4 = mybir.dt.float8_e4m3fn_x4
+FP4X4 = mybir.dt.float4_e2m1fn_x4
+ACT = mybir.ActivationFunctionType
+ALU = mybir.AluOpType
+
+P = 128
+PACK = 4
+K_PASS = P * PACK
+PASSES = K // K_PASS
+BANK = 512
+HALVES = S // BANK
+CHUNK = BANK // PACK
+CHUNKS = S // CHUNK
+M_TILES = S2 // P
+QUADS = 4
+LIST_ROWS = 16
+
+
+def tile_list_claimant_record_scores_kernel(
+    tc, tab_words, tab_scales, offs, tab2_words, tab2_scales, offs2, pos1, pos2,
+    w1, gain, w2_words, w2_scales, b2, w3, vec, shift, out,
+):
+    nc = tc.nc
+    with ExitStack() as ctx:
+        keep = ctx.enter_context(tc.tile_pool(name="keep", bufs=1))
+        work = ctx.enter_context(tc.tile_pool(name="work", bufs=3))
+        psum = ctx.enter_context(tc.psum_pool(name="psum", bufs=8))
+
+        def held(shape, dtype, name, after=None):
+            return keep.tile(shape, dtype, name=name, tag=after or name, align_bytes=64)
+
+        def bank(shape):
+            return psum.tile(shape, F32, name="bank")
+
+        offs_sb = keep.tile([P, S // LIST_ROWS], U16, name="offs_sb")
+        offs2_sb = keep.tile([P, S2 // LIST_ROWS], U16, name="offs2_sb")
+        pos1_sb = keep.tile([P, NP // LIST_ROWS], U16, name="pos1_sb")
+        pos2_sb = keep.tile([P, NP // LIST_ROWS], U16, name="pos2_sb")
+
+        tab_sc = held([P, T], U8, "tab_sc")
+        w2_sc_raw = held([P, PASSES, H], U8, "w2_sc_raw")
+        tab2_sc = held([P, T3], U8, "tab2_sc")
+        v_sc = [held([P, S], U8, f"v_sc{a}") for a in range(PASSES)]
+        first_live = 32 - 4 * PASSES
+        nc.vector.memset(w2_sc_raw[:].bitcast(I32), 0)
+        nc.vector.memset(tab2_sc[:].bitcast(I32), 0)
+        for q in range(QUADS):
+            nc.vector.memset(tab_sc[32 * q : 32 * q + first_live, :].bitcast(I32), 0)
+        for a in range(PASSES):
+            nc.vector.memset(v_sc[a][96:P, :].bitcast(I32), 0)
+
+        nc.sync.dma_start(offs_sb[:], offs)
+        for q in range(QUADS):
+            nc.sync.dma_start(
+                tab_sc[32 * q + first_live : 32 * (q + 1), :].bitcast(I32),
+                tab_scales[:, 4 * q : 4 * q + 4, :].bitcast(I32),
+            )
+        w2_raw = held([P, PASSES, 2 * H], U8, "w2_raw")
+        nc.sync.dma_start(w2_raw[:].bitcast(I32), w2_words.rearrange("a p c -> p a c").bitcast(I32))
+        for q in range(QUADS):
+            nc.sync.dma_start(
+                w2_sc_raw[32 * q : 32 * q + 4, :, :].bitcast(I32),
+                w2_scales[:, 4 * q : 4 * q + 4, :].rearrange("a r c -> r a c").bitcast(I32),
+            )
+
+        def table_words(words):
+            return words.rearrange("p t i -> p (t i)").bitcast(I32)
+
+        tab_w = [held([P, T], I32, "tab_w0"), held([P, T], I32, "tab_w1", after="w2_raw")]
+        nc.sync.dma_start(tab_w[0][:], table_words(tab_words[0]))
+        nc.sync.dma_start(offs2_sb[:], offs2)
+        for q in range(QUADS):
+            nc.sync.dma_start(
+                tab2_sc[32 * q : 32 * q + 4, :].bitcast(I32),
+                tab2_scales[0, 4 * q : 4 * q + 4, :].bitcast(I32),
+            )
+        b2_sb = held([P, PACK], F32, "b2_sb")
+        gain_sb = held([P, PACK], F32, "gain_sb")
+        nc.sync.dma_start(b2_sb[:], b2.rearrange("(p t) -> p t", t=PACK))
+        nc.sync.dma_start(gain_sb[:], gain.rearrange("(p t) -> p t", t=PACK))
+        nc.sync.dma_start(pos1_sb[:], pos1)
+        nc.sync.dma_start(pos2_sb[:], pos2)
+
+        w2_w = held([P, PASSES, 2 * H], U8, "w2_w")
+        w2_sc = held([P, PASSES, H], U8, "w2_sc")
+        nc.vector.tensor_copy(
+            w2_w[:].bitcast(U16).rearrange("p a (t q) -> p a q t", t=PACK),
+            w2_raw[:].bitcast(U16).rearrange("p a (q t) -> p a q t", t=PACK),
+        )
+        nc.vector.tensor_copy(
+            w2_sc[:].rearrange("p a (t q) -> p a q t", t=PACK),
+            w2_sc_raw[:].rearrange("p a (q t) -> p a q t", t=PACK),
+        )
+
+        nc.sync.dma_start(tab_w[1][:], table_words(tab_words[1]))
+
+        v_sc_both = held([P, S], U8, "v_sc_both")
+        nc.vector.tensor_copy(v_sc_both[:], tab_sc[:].indirect(offs_sb[:]))
+        live = 32 * (QUADS - 1) + 4
+        for a in range(PASSES):
+            first = first_live + 4 * a
+            nc.scalar.dma_start(v_sc[a][0:live, :].bitcast(I32), v_sc_both[first : first + live, :].bitcast(I32))
+
+        def load_w1(a, after):
+            raw = held([P, PACK, H], F32, f"w1_raw{a}", after=after)
+            nc.sync.dma_start(raw[:], w1[a * K_PASS : (a + 1) * K_PASS, :].rearrange("(p j) c -> p j c", j=PACK))
+            return raw
+
+        w1_raw = [load_w1(0, "tab_sc")]
+
+        cols = BANK // LIST_ROWS
+        v_w = [[held([P, BANK], U32, f"v_w{a}{u}") for u in range(HALVES)] for a in range(PASSES)]
+
+        def gather_records(a):
+            for u in range(HALVES):
+                nc.vector.tensor_copy(
+                    v_w[a][u][:], tab_w[a][:].bitcast(U32).indirect(offs_sb[:, u * cols : (u + 1) * cols])
+                )
+
+        def records(a, c):
+            u, first = divmod(c * CHUNK, BANK)
+            return v_w[a][u][:, first : first + CHUNK].bitcast(FP8X4)
+
+        v2_sc = held([P, S2], U8, "v2_sc")
+        gather_records(0)
+        w1_raw.append(load_w1(1, "tab_w0"))
+        nc.vector.tensor_copy(v2_sc[:], tab2_sc[:].indirect(offs2_sb[:]))
+        gather_records(1)
+        tab2_w = held([P, T3], I32, "tab2_w", after="w2_raw")
+        nc.sync.dma_start(tab2_w[:], table_words(tab2_words[0]))
+
+        g_banks = [bank([P, PACK, CHUNK]) for c in range(CHUNKS)]
+        for a in range(PASSES):
+            for c in range(CHUNKS):
+                for t in range(PACK):
+                    nc.tensor.matmul_mx(
+                        out=g_banks[c][:, t, :],
+                        lhsT=w2_w[:, a, 2 * P * t : 2 * P * (t + 1)].bitcast(FP4X4),
+                        lhsT_scale=w2_sc[:, a, P * t : P * (t + 1)],
+                        rhs=records(a, c),
+                        rhs_scale=v_sc[a][:, c * CHUNK : (c + 1) * CHUNK],
+                        start=(a == 0 and t == 0),
+                        stop=(a == PASSES - 1 and t == PACK - 1),
+                    )
+
+        def quantised(name, width):
+            return held([P, width], U32, f"{name}_w"), held([P, width], U8, f"{name}_sc")
+
+        def quantise(dst, src):
+            nc.vector.quantize_mx(out=dst[0][:].bitcast(FP8X4), scales=dst[1][:], in_=src)
+
+        def per_slot(values):
+            return values[:].unsqueeze(1).to_broadcast([P, CHUNK, PACK])
+
+        per_half = CHUNKS // HALVES
+        g_bf = [held([P, BANK, PACK], BF16, f"g_bf{u}") for u in range(HALVES)]
+        gq = [quantised(f"gq{u}", BANK) for u in range(HALVES)]
+        for c in range(CHUNKS):
+            u, first = divmod(c * CHUNK, BANK)
+            nc.vector.tensor_tensor(
+                g_bf[u][:, first : first + CHUNK, :],
+                g_banks[c][:].rearrange("p t n -> p n t"),
+                per_slot(b2_sb),
+                ALU.add,
+            )
+            if c == per_half:
+                quantise(gq[0], g_bf[0][:].rearrange("p n t -> p (n t)"))
+
+        w3_raw = []
+        w1q = [quantised(f"w1q{a}", H) for a in range(PASSES)]
+        for a in range(PASSES):
+            w1_bf = held([P, H * PACK], BF16, f"w1_bf{a}")
+            nc.scalar.activation(
+                w1_bf[:].rearrange("p (t m j) -> p m j t", t=PACK, j=PACK),
+                w1_raw[a][:].rearrange("p j (m t) -> p m j t", t=PACK),
+                ACT.Copy,
+            )
+            quantise(w1q[a], w1_bf[:])
+            w3_raw.append(held([P, PACK, BANK], F32, f"w3_raw{a}", after=("tab_sc", "tab_w0")[a]))
+            nc.sync.dma_start(
+                w3_raw[a][:], w3[:, a * BANK : (a + 1) * BANK].rearrange("(p j) c -> p j c", j=PACK)
+            )
+        quantise(gq[1], g_bf[1][:].rearrange("p n t -> p (n t)"))
+
+        v2_w = held([P, S2], U32, "v2_w")
+        nc.vector.tensor_copy(v2_w[:], tab2_w[:].bitcast(U32).indirect(offs2_sb[:]))
+
+        shift_rows = shift.rearrange("(i p) n -> p i n", p=P)
+        shift_sb = [held([P, M_TILES // 2, NP], F32, "shift_sb0", after="w2_raw")]
+        nc.sync.dma_start(shift_sb[0][:], shift_rows[:, : M_TILES // 2, :])
+        vec_sb = held([P, M_TILES], F32, "vec_sb", after="w1_bf1")
+        with nc.allow_non_contiguous_dma(reason="one value of vec for each row of a tile of claimants"):
+            nc.sync.dma_start(vec_sb[:], vec.rearrange("(i p) -> p i", p=P))
+
+        h_bf = [held([P, BANK, PACK], BF16, f"h_bf{u}") for u in range(HALVES)]
+        hq = [quantised(f"hq{u}", BANK) for u in range(HALVES)]
+        for c in range(CHUNKS):
+            u, first = divmod(c * CHUNK, BANK)
+            acc = bank([P, PACK, CHUNK])
+            for a in range(PASSES):
+                for t in range(PACK):
+                    nc.tensor.matmul_mx(
+                        out=acc[:, t, :],
+                        lhsT=w1q[a][0][:, P * t : P * (t + 1)].bitcast(FP8X4),
+                        lhsT_scale=w1q[a][1][:, P * t : P * (t + 1)],
+                        rhs=records(a, c),
+                        rhs_scale=v_sc[a][:, c * CHUNK : (c + 1) * CHUNK],
+                        start=(a == 0 and t == 0),
+                        stop=(a == PASSES - 1 and t == PACK - 1),
+                    )
+            th = work.tile([P, CHUNK, PACK], F32, name="th", bufs=4)
+            nc.scalar.activation(th[:], acc[:].rearrange("p t n -> p n t"), ACT.Tanh)
+            nc.vector.tensor_tensor(h_bf[u][:, first : first + CHUNK, :], th[:], per_slot(gain_sb), ALU.mult)
+            if c == per_half:
+                quantise(hq[0], h_bf[0][:].rearrange("p n t -> p (n t)"))
+
+        w3q = [quantised(f"w3q{u}", BANK) for u in range(S2 // BANK)]
+
+        def quantise_w3(u):
+            w3_bf = held([P, BANK * PACK], BF16, f"w3_bf{u}")
+            nc.scalar.activation(
+                w3_bf[:].rearrange("p (c i j) -> p c j i", i=4, j=PACK),
+                w3_raw[u][:].rearrange("p j (c i) -> p c j i", i=4),
+                ACT.Copy,
+            )
+            quantise(w3q[u], w3_bf[:])
+
+        quantise_w3(0)
+        shift_sb.append(held([P, M_TILES // 2, NP], F32, "shift_sb1", after="tab_sc"))
+        nc.sync.dma_start(shift_sb[1][:], shift_rows[:, M_TILES // 2 :, :])
+        quantise(hq[1], h_bf[1][:].rearrange("p n t -> p (n t)"))
+
+        def product(weights, weight_scales, operand):
+            acc = bank([P, BANK])
+            nc.tensor.matmul_mx(
+                out=acc[:], lhsT=weights.bitcast(FP8X4), lhsT_scale=weight_scales,
+                rhs=operand[0][:].bitcast(FP8X4), rhs_scale=operand[1][:], start=True, stop=True,
+            )
+            return acc
+
+        def rows(i):
+            return slice(i * P, (i + 1) * P)
+
+        def half(u):
+            return slice(u * BANK, (u + 1) * BANK)
+
+        def scores_e(i, u, e, top, top_so_far):
+            acc = product(v2_w[:, rows(i)], v2_sc[:, rows(i)], hq[u])
+            nc.vector.tensor_scalar(e[:, half(u)], acc[:], 1.0, top_so_far, ALU.mult, ALU.max, accum_out=top)
+
+        def look(e, top):
+            neg_top = work.tile([P, 1], F32, name="neg_top")
+            nc.scalar.activation(neg_top[:], top, ACT.Copy, scale=-1.0)
+            a = work.tile([P, NP], F32, name="a")
+            nc.scalar.activation(a[:], e[:].indirect(pos1_sb[:]), ACT.Exp, bias=neg_top[:])
+            return a
+
+        def scores_w3(i):
+            w, first = divmod(i * P, BANK)
+            d2 = work.tile([P, S], F32, name="d2")
+            for u in range(HALVES):
+                acc = product(w3q[w][0][:, first : first + P], w3q[w][1][:, first : first + P], gq[u])
+                nc.scalar.copy(d2[:, half(u)], acc[:])
+            return d2
+
+        def scores_d(i, u, d, d2):
+            acc = product(v2_w[:, rows(i)], v2_sc[:, rows(i)], gq[u])
+            nc.vector.tensor_tensor(d[:, half(u)], acc[:], d2[:, half(u)], ALU.max)
+
+        def weigh(i, a):
+            c = work.tile([P, NP], F32, name="c")
+            part, place = divmod(i, M_TILES // 2)
+            nc.vector.scalar_tensor_tensor(
+                c[:], a[:], vec_sb[:, i : i + 1], shift_sb[part][:, place, :], ALU.mult, ALU.add
+            )
+            return c
+
+        def finish(i, d, c):
+            o = work.tile([P, NP], F32, name="o")
+            nc.vector.tensor_tensor(o[:], d[:].indirect(pos2_sb[:]), c[:], ALU.mult)
+            nc.sync.dma_start(out[rows(i), :], o[:])
+
+        d2 = scores_w3(0)
+        for i in range(M_TILES):
+            e = work.tile([P, S], F32, name="e", bufs=2)
+            d = work.tile([P, S], F32, name="d")
+            tops = work.tile([P, HALVES], F32, name="tops")
+            scores_e(i, 0, e, tops[:, 0:1], None)
+            scores_d(i, 0, d, d2)
+            scores_e(i, 1, e, tops[:, 1:2], tops[:, 0:1])
+            if i > 0:
+                c = weigh(i - 1, a)
+            scores_d(i, 1, d, d2)
+            if i == 1:
+                quantise_w3(1)
+            if i + 1 < M_TILES:
+                d2 = scores_w3(i + 1)
+            a = look(e, tops[:, 1:2])
+            if i > 0:
+                finish(i - 1, d_before, c)
+            d_before = d
+        finish(M_TILES - 1, d_before, weigh(M_TILES - 1, a))

@@ -54,13 +54,18 @@ def tile_list_claimant_record_scores_kernel(
         w2_sc_raw = held([P, PASSES, H], U8, "w2_sc_raw")
         tab2_sc = held([P, T3], U8, "tab2_sc")
         v_sc = [held([P, S], U8, f"v_sc{a}") for a in range(PASSES)]
+        v2_sc = held([P, S2], U8, "v2_sc")
         first_live = 32 - 4 * PASSES
-        nc.vector.memset(w2_sc_raw[:].bitcast(I32), 0)
-        nc.vector.memset(tab2_sc[:].bitcast(I32), 0)
+        first_live2 = 32 - 4
+        nc.gpsimd.memset(w2_sc_raw[:].bitcast(I32), 0)
         for q in range(QUADS):
-            nc.vector.memset(tab_sc[32 * q : 32 * q + first_live, :].bitcast(I32), 0)
-        for a in range(PASSES):
-            nc.vector.memset(v_sc[a][96:P, :].bitcast(I32), 0)
+            engine = nc.vector if q < QUADS // 2 else nc.gpsimd
+            engine.memset(tab_sc[32 * q : 32 * q + first_live, :].bitcast(I32), 0)
+        for plane in v_sc:
+            nc.gpsimd.memset(plane[96:P, :].bitcast(I32), 0)
+        for q in range(QUADS):
+            nc.gpsimd.memset(tab2_sc[32 * q : 32 * q + first_live2, :].bitcast(I32), 0)
+        nc.gpsimd.memset(v2_sc[96:P, :].bitcast(I32), 0)
 
         nc.sync.dma_start(offs_sb[:], offs)
         for q in range(QUADS):
@@ -68,6 +73,18 @@ def tile_list_claimant_record_scores_kernel(
                 tab_sc[32 * q + first_live : 32 * (q + 1), :].bitcast(I32),
                 tab_scales[:, 4 * q : 4 * q + 4, :].bitcast(I32),
             )
+        nc.sync.dma_start(offs2_sb[:], offs2)
+        for q in range(QUADS):
+            nc.sync.dma_start(
+                tab2_sc[32 * q + first_live2 : 32 * (q + 1), :].bitcast(I32),
+                tab2_scales[0, 4 * q : 4 * q + 4, :].bitcast(I32),
+            )
+
+        def table_words(words):
+            return words.rearrange("p t i -> p (t i)").bitcast(I32)
+
+        tab_w = [held([P, T], I32, f"tab_w{a}") for a in range(PASSES)]
+        nc.sync.dma_start(tab_w[0][:], table_words(tab_words[0]))
         w2_raw = held([P, PASSES, 2 * H], U8, "w2_raw")
         nc.sync.dma_start(w2_raw[:].bitcast(I32), w2_words.rearrange("a p c -> p a c").bitcast(I32))
         for q in range(QUADS):
@@ -75,51 +92,33 @@ def tile_list_claimant_record_scores_kernel(
                 w2_sc_raw[32 * q : 32 * q + 4, :, :].bitcast(I32),
                 w2_scales[:, 4 * q : 4 * q + 4, :].rearrange("a r c -> r a c").bitcast(I32),
             )
-
-        def table_words(words):
-            return words.rearrange("p t i -> p (t i)").bitcast(I32)
-
-        tab_w = [held([P, T], I32, "tab_w0"), held([P, T], I32, "tab_w1", after="w2_raw")]
-        nc.sync.dma_start(tab_w[0][:], table_words(tab_words[0]))
-        nc.sync.dma_start(offs2_sb[:], offs2)
-        for q in range(QUADS):
-            nc.sync.dma_start(
-                tab2_sc[32 * q : 32 * q + 4, :].bitcast(I32),
-                tab2_scales[0, 4 * q : 4 * q + 4, :].bitcast(I32),
-            )
         b2_sb = held([P, PACK], F32, "b2_sb")
         gain_sb = held([P, PACK], F32, "gain_sb")
         nc.sync.dma_start(b2_sb[:], b2.rearrange("(p t) -> p t", t=PACK))
-        nc.sync.dma_start(gain_sb[:], gain.rearrange("(p t) -> p t", t=PACK))
-        nc.sync.dma_start(pos1_sb[:], pos1)
-        nc.sync.dma_start(pos2_sb[:], pos2)
-
-        w2_w = held([P, PASSES, 2 * H], U8, "w2_w")
-        w2_sc = held([P, PASSES, H], U8, "w2_sc")
-        nc.vector.tensor_copy(
-            w2_w[:].bitcast(U16).rearrange("p a (t q) -> p a q t", t=PACK),
-            w2_raw[:].bitcast(U16).rearrange("p a (q t) -> p a q t", t=PACK),
-        )
-        nc.vector.tensor_copy(
-            w2_sc[:].rearrange("p a (t q) -> p a q t", t=PACK),
-            w2_sc_raw[:].rearrange("p a (q t) -> p a q t", t=PACK),
-        )
-
         nc.sync.dma_start(tab_w[1][:], table_words(tab_words[1]))
-
-        v_sc_both = held([P, S], U8, "v_sc_both")
-        nc.vector.tensor_copy(v_sc_both[:], tab_sc[:].indirect(offs_sb[:]))
-        live = 32 * (QUADS - 1) + 4
-        for a in range(PASSES):
-            first = first_live + 4 * a
-            nc.scalar.dma_start(v_sc[a][0:live, :].bitcast(I32), v_sc_both[first : first + live, :].bitcast(I32))
 
         def load_w1(a, after):
             raw = held([P, PACK, H], F32, f"w1_raw{a}", after=after)
             nc.sync.dma_start(raw[:], w1[a * K_PASS : (a + 1) * K_PASS, :].rearrange("(p j) c -> p j c", j=PACK))
             return raw
 
-        w1_raw = [load_w1(0, "tab_sc")]
+        w1_raw = [load_w1(0, None)]
+        nc.sync.dma_start(gain_sb[:], gain.rearrange("(p t) -> p t", t=PACK))
+        nc.sync.dma_start(pos1_sb[:], pos1)
+        nc.sync.dma_start(pos2_sb[:], pos2)
+
+        live = 32 * (QUADS - 1) + 4
+
+        def to_row_0(plane, gathered, first):
+            nc.scalar.dma_start(plane[0:live, :].bitcast(I32), gathered[first : first + live, :].bitcast(I32))
+
+        v_sc_both = held([P, S], U8, "v_sc_both")
+        nc.vector.tensor_copy(v_sc_both[:], tab_sc[:].indirect(offs_sb[:]))
+        for a in range(PASSES):
+            to_row_0(v_sc[a], v_sc_both, first_live + 4 * a)
+        v2_sc_low = held([P, S2], U8, "v2_sc_low")
+        nc.vector.tensor_copy(v2_sc_low[:], tab2_sc[:].indirect(offs2_sb[:]))
+        to_row_0(v2_sc, v2_sc_low, first_live2)
 
         cols = BANK // LIST_ROWS
         v_w = [[held([P, BANK], U32, f"v_w{a}{u}") for u in range(HALVES)] for a in range(PASSES)]
@@ -134,27 +133,46 @@ def tile_list_claimant_record_scores_kernel(
             u, first = divmod(c * CHUNK, BANK)
             return v_w[a][u][:, first : first + CHUNK].bitcast(FP8X4)
 
-        v2_sc = held([P, S2], U8, "v2_sc")
+        w2_w = held([P, PASSES, 2 * H], U8, "w2_w")
+        w2_sc = held([P, PASSES, H], U8, "w2_sc")
+        nc.vector.tensor_copy(
+            w2_w[:].bitcast(U16).rearrange("p a (t q) -> p a t q", t=PACK),
+            w2_raw[:].bitcast(U16).rearrange("p a (q t) -> p a t q", t=PACK),
+        )
+        nc.vector.tensor_copy(
+            w2_sc[:].rearrange("p a (t q) -> p a t q", t=PACK),
+            w2_sc_raw[:].rearrange("p a (q t) -> p a t q", t=PACK),
+        )
+
         gather_records(0)
         w1_raw.append(load_w1(1, "tab_w0"))
-        nc.vector.tensor_copy(v2_sc[:], tab2_sc[:].indirect(offs2_sb[:]))
         gather_records(1)
-        tab2_w = held([P, T3], I32, "tab2_w", after="w2_raw")
-        nc.sync.dma_start(tab2_w[:], table_words(tab2_words[0]))
+
+        def load_w3(u, after):
+            raw = held([P, PACK, BANK], F32, f"w3_raw{u}", after=after)
+            nc.sync.dma_start(raw[:], w3[:, u * BANK : (u + 1) * BANK].rearrange("(p j) c -> p j c", j=PACK))
+            return raw
+
+        w3_raw = [load_w3(0, "tab_w1")]
 
         g_banks = [bank([P, PACK, CHUNK]) for c in range(CHUNKS)]
-        for a in range(PASSES):
-            for c in range(CHUNKS):
-                for t in range(PACK):
-                    nc.tensor.matmul_mx(
-                        out=g_banks[c][:, t, :],
-                        lhsT=w2_w[:, a, 2 * P * t : 2 * P * (t + 1)].bitcast(FP4X4),
-                        lhsT_scale=w2_sc[:, a, P * t : P * (t + 1)],
-                        rhs=records(a, c),
-                        rhs_scale=v_sc[a][:, c * CHUNK : (c + 1) * CHUNK],
-                        start=(a == 0 and t == 0),
-                        stop=(a == PASSES - 1 and t == PACK - 1),
-                    )
+
+        def g_pass(a, c):
+            for t in range(PACK):
+                nc.tensor.matmul_mx(
+                    out=g_banks[c][:, t, :],
+                    lhsT=w2_w[:, a, 2 * P * t : 2 * P * (t + 1)].bitcast(FP4X4),
+                    lhsT_scale=w2_sc[:, a, P * t : P * (t + 1)],
+                    rhs=records(a, c),
+                    rhs_scale=v_sc[a][:, c * CHUNK : (c + 1) * CHUNK],
+                    start=(a == 0 and t == 0),
+                    stop=(a == PASSES - 1 and t == PACK - 1),
+                )
+
+        for c in range(CHUNKS):
+            g_pass(0, c)
+        for c in range(CHUNKS):
+            g_pass(1, c)
 
         def quantised(name, width):
             return held([P, width], U32, f"{name}_w"), held([P, width], U8, f"{name}_sc")
@@ -164,6 +182,17 @@ def tile_list_claimant_record_scores_kernel(
 
         def per_slot(values):
             return values[:].unsqueeze(1).to_broadcast([P, CHUNK, PACK])
+
+        w1q = [quantised(f"w1q{a}", H) for a in range(PASSES)]
+
+        def quantise_w1(a):
+            w1_bf = held([P, H * PACK], BF16, f"w1_bf{a}")
+            nc.scalar.activation(
+                w1_bf[:].rearrange("p (t m j) -> p m j t", t=PACK, j=PACK),
+                w1_raw[a][:].rearrange("p j (m t) -> p m j t", t=PACK),
+                ACT.Copy,
+            )
+            quantise(w1q[a], w1_bf[:])
 
         per_half = CHUNKS // HALVES
         g_bf = [held([P, BANK, PACK], BF16, f"g_bf{u}") for u in range(HALVES)]
@@ -176,32 +205,39 @@ def tile_list_claimant_record_scores_kernel(
                 per_slot(b2_sb),
                 ALU.add,
             )
+            if c == per_half - 1:
+                quantise_w1(0)
             if c == per_half:
                 quantise(gq[0], g_bf[0][:].rearrange("p n t -> p (n t)"))
 
-        w3_raw = []
-        w1q = [quantised(f"w1q{a}", H) for a in range(PASSES)]
-        for a in range(PASSES):
-            w1_bf = held([P, H * PACK], BF16, f"w1_bf{a}")
-            nc.scalar.activation(
-                w1_bf[:].rearrange("p (t m j) -> p m j t", t=PACK, j=PACK),
-                w1_raw[a][:].rearrange("p j (m t) -> p m j t", t=PACK),
-                ACT.Copy,
-            )
-            quantise(w1q[a], w1_bf[:])
-            w3_raw.append(held([P, PACK, BANK], F32, f"w3_raw{a}", after=("tab_sc", "tab_w0")[a]))
-            nc.sync.dma_start(
-                w3_raw[a][:], w3[:, a * BANK : (a + 1) * BANK].rearrange("(p j) c -> p j c", j=PACK)
-            )
+        tab2_w = held([P, T3], I32, "tab2_w", after="w1_raw0")
+        nc.sync.dma_start(tab2_w[:], table_words(tab2_words[0]))
+
+        def h_pass(acc, a, c):
+            for t in range(PACK):
+                nc.tensor.matmul_mx(
+                    out=acc[:, t, :],
+                    lhsT=w1q[a][0][:, P * t : P * (t + 1)].bitcast(FP8X4),
+                    lhsT_scale=w1q[a][1][:, P * t : P * (t + 1)],
+                    rhs=records(a, c),
+                    rhs_scale=v_sc[a][:, c * CHUNK : (c + 1) * CHUNK],
+                    start=(a == 0 and t == 0),
+                    stop=(a == PASSES - 1 and t == PACK - 1),
+                )
+
+        h_banks = [bank([P, PACK, CHUNK]) for c in range(per_half)]
+        for c in range(per_half):
+            h_pass(h_banks[c], 0, c)
+
+        quantise_w1(1)
+        w3_raw.append(load_w3(1, "tab_w0"))
         quantise(gq[1], g_bf[1][:].rearrange("p n t -> p (n t)"))
 
-        v2_w = held([P, S2], U32, "v2_w")
+        v2_w = held([P, S2], U32, "v2_w", after="w1_bf1")
         nc.vector.tensor_copy(v2_w[:], tab2_w[:].bitcast(U32).indirect(offs2_sb[:]))
 
         shift_rows = shift.rearrange("(i p) n -> p i n", p=P)
-        shift_sb = [held([P, M_TILES // 2, NP], F32, "shift_sb0", after="w2_raw")]
-        nc.sync.dma_start(shift_sb[0][:], shift_rows[:, : M_TILES // 2, :])
-        vec_sb = held([P, M_TILES], F32, "vec_sb", after="w1_bf1")
+        vec_sb = held([P, M_TILES], F32, "vec_sb", after="w1_bf0")
         with nc.allow_non_contiguous_dma(reason="one value of vec for each row of a tile of claimants"):
             nc.sync.dma_start(vec_sb[:], vec.rearrange("(i p) -> p i", p=P))
 
@@ -209,19 +245,13 @@ def tile_list_claimant_record_scores_kernel(
         hq = [quantised(f"hq{u}", BANK) for u in range(HALVES)]
         for c in range(CHUNKS):
             u, first = divmod(c * CHUNK, BANK)
-            acc = bank([P, PACK, CHUNK])
-            for a in range(PASSES):
-                for t in range(PACK):
-                    nc.tensor.matmul_mx(
-                        out=acc[:, t, :],
-                        lhsT=w1q[a][0][:, P * t : P * (t + 1)].bitcast(FP8X4),
-                        lhsT_scale=w1q[a][1][:, P * t : P * (t + 1)],
-                        rhs=records(a, c),
-                        rhs_scale=v_sc[a][:, c * CHUNK : (c + 1) * CHUNK],
-                        start=(a == 0 and t == 0),
-                        stop=(a == PASSES - 1 and t == PACK - 1),
-                    )
-            th = work.tile([P, CHUNK, PACK], F32, name="th", bufs=4)
+            if c < per_half:
+                acc = h_banks[c]
+            else:
+                acc = bank([P, PACK, CHUNK])
+                h_pass(acc, 0, c)
+            h_pass(acc, 1, c)
+            th = work.tile([P, CHUNK, PACK], F32, name="th", bufs=CHUNKS)
             nc.scalar.activation(th[:], acc[:].rearrange("p t n -> p n t"), ACT.Tanh)
             nc.vector.tensor_tensor(h_bf[u][:, first : first + CHUNK, :], th[:], per_slot(gain_sb), ALU.mult)
             if c == per_half:
@@ -229,19 +259,23 @@ def tile_list_claimant_record_scores_kernel(
 
         w3q = [quantised(f"w3q{u}", BANK) for u in range(S2 // BANK)]
 
-        def quantise_w3(u):
-            w3_bf = held([P, BANK * PACK], BF16, f"w3_bf{u}")
+        w3_bf = [held([P, BANK * PACK], BF16, f"w3_bf{u}") for u in range(S2 // BANK)]
+        piece = BANK // 2
+
+        def round_w3(u, v):
             nc.scalar.activation(
-                w3_bf[:].rearrange("p (c i j) -> p c j i", i=4, j=PACK),
-                w3_raw[u][:].rearrange("p j (c i) -> p c j i", i=4),
+                w3_bf[u][:, v * piece * PACK : (v + 1) * piece * PACK].rearrange("p (c i j) -> p c j i", i=4, j=PACK),
+                w3_raw[u][:, :, v * piece : (v + 1) * piece].rearrange("p j (c i) -> p c j i", i=4),
                 ACT.Copy,
             )
-            quantise(w3q[u], w3_bf[:])
 
-        quantise_w3(0)
-        shift_sb.append(held([P, M_TILES // 2, NP], F32, "shift_sb1", after="tab_sc"))
+        round_w3(0, 0)
+        round_w3(0, 1)
+        quantise(w3q[0], w3_bf[0][:])
+        shift_sb = [held([P, M_TILES // 2, NP], F32, "shift_sb0", after="tab_w1")]
+        nc.sync.dma_start(shift_sb[0][:], shift_rows[:, : M_TILES // 2, :])
+        shift_sb.append(held([P, M_TILES // 2, NP], F32, "shift_sb1", after="w1_raw0"))
         nc.sync.dma_start(shift_sb[1][:], shift_rows[:, M_TILES // 2 :, :])
-        quantise(hq[1], h_bf[1][:].rearrange("p n t -> p (n t)"))
 
         def product(weights, weight_scales, operand):
             acc = bank([P, BANK])
@@ -283,9 +317,9 @@ def tile_list_claimant_record_scores_kernel(
         def weigh(i, a):
             c = work.tile([P, NP], F32, name="c")
             part, place = divmod(i, M_TILES // 2)
-            nc.vector.scalar_tensor_tensor(
-                c[:], a[:], vec_sb[:, i : i + 1], shift_sb[part][:, place, :], ALU.mult, ALU.add
-            )
+            scaled = work.tile([P, NP], F32, name="scaled")
+            nc.scalar.activation(scaled[:], a[:], ACT.Copy, scale=vec_sb[:, i : i + 1])
+            nc.gpsimd.tensor_tensor(c[:], scaled[:], shift_sb[part][:, place, :], ALU.add)
             return c
 
         def finish(i, d, c):
@@ -293,23 +327,38 @@ def tile_list_claimant_record_scores_kernel(
             nc.vector.tensor_tensor(o[:], d[:].indirect(pos2_sb[:]), c[:], ALU.mult)
             nc.sync.dma_start(out[rows(i), :], o[:])
 
-        d2 = scores_w3(0)
-        for i in range(M_TILES):
+        def first_scores(i):
             e = work.tile([P, S], F32, name="e", bufs=2)
-            d = work.tile([P, S], F32, name="d")
             tops = work.tile([P, HALVES], F32, name="tops")
             scores_e(i, 0, e, tops[:, 0:1], None)
-            scores_d(i, 0, d, d2)
+            return e, tops
+
+        def last_scores(i, e, tops):
             scores_e(i, 1, e, tops[:, 1:2], tops[:, 0:1])
-            if i > 0:
-                c = weigh(i - 1, a)
-            scores_d(i, 1, d, d2)
-            if i == 1:
-                quantise_w3(1)
+            return e, tops[:, 1:2]
+
+        begun = first_scores(0)
+        quantise(hq[1], h_bf[1][:].rearrange("p n t -> p (n t)"))
+        begun_next = first_scores(1)
+        weights = [weigh(0, look(*last_scores(0, *begun)))]
+        scored = last_scores(1, *begun_next)
+        second = [scores_w3(0), scores_w3(1)]
+        round_w3(1, 0)
+        round_w3(1, 1)
+        loss = []
+        for i in range(M_TILES):
+            d = work.tile([P, S], F32, name="d")
+            for u in range(HALVES):
+                scores_d(i, u, d, second[i])
+            loss.append(d)
+            if i == 0:
+                quantise(w3q[1], w3_bf[1][:])
             if i + 1 < M_TILES:
-                d2 = scores_w3(i + 1)
-            a = look(e, tops[:, 1:2])
+                weights.append(weigh(i + 1, look(*scored)))
+            if i + 2 < M_TILES:
+                second.append(scores_w3(i + 2))
             if i > 0:
-                finish(i - 1, d_before, c)
-            d_before = d
-        finish(M_TILES - 1, d_before, weigh(M_TILES - 1, a))
+                finish(i - 1, loss[i - 1], weights[i - 1])
+            if i + 2 < M_TILES:
+                scored = last_scores(i + 2, *first_scores(i + 2))
+        finish(M_TILES - 1, loss[-1], weights[-1])

@@ -87,10 +87,10 @@ def tile_list_claimant_record_scores_kernel(
         nc.sync.dma_start(tab_w[0][:], table_words(tab_words[0]))
         w2_raw = held([P, PASSES, 2 * H], U8, "w2_raw")
         nc.sync.dma_start(w2_raw[:].bitcast(I32), w2_words.rearrange("a p c -> p a c").bitcast(I32))
-        for q in range(QUADS):
+        for r in range(4):
             nc.sync.dma_start(
-                w2_sc_raw[32 * q : 32 * q + 4, :, :].bitcast(I32),
-                w2_scales[:, 4 * q : 4 * q + 4, :].rearrange("a r c -> r a c").bitcast(I32),
+                w2_sc_raw[r : P : 32, :, :].bitcast(I32),
+                w2_scales[:, r : 16 : 4, :].rearrange("a q c -> q a c").bitcast(I32),
             )
         b2_sb = held([P, PACK], F32, "b2_sb")
         gain_sb = held([P, PACK], F32, "gain_sb")
@@ -180,16 +180,16 @@ def tile_list_claimant_record_scores_kernel(
         def quantise(dst, src):
             nc.vector.quantize_mx(out=dst[0][:].bitcast(FP8X4), scales=dst[1][:], in_=src)
 
-        def per_slot(values):
-            return values[:].unsqueeze(1).to_broadcast([P, CHUNK, PACK])
+        def per_slot(values, columns):
+            return values[:].unsqueeze(1).to_broadcast([P, columns, PACK])
 
         w1q = [quantised(f"w1q{a}", H) for a in range(PASSES)]
 
         def quantise_w1(a):
             w1_bf = held([P, H * PACK], BF16, f"w1_bf{a}")
             nc.scalar.activation(
-                w1_bf[:].rearrange("p (t m j) -> p m j t", t=PACK, j=PACK),
-                w1_raw[a][:].rearrange("p j (m t) -> p m j t", t=PACK),
+                w1_bf[:].rearrange("p (t m j) -> p m t j", t=PACK, j=PACK),
+                w1_raw[a][:].rearrange("p j (m t) -> p m t j", t=PACK),
                 ACT.Copy,
             )
             quantise(w1q[a], w1_bf[:])
@@ -202,7 +202,7 @@ def tile_list_claimant_record_scores_kernel(
             nc.vector.tensor_tensor(
                 g_bf[u][:, first : first + CHUNK, :],
                 g_banks[c][:].rearrange("p t n -> p n t"),
-                per_slot(b2_sb),
+                per_slot(b2_sb, CHUNK),
                 ALU.add,
             )
             if c == per_half - 1:
@@ -237,25 +237,6 @@ def tile_list_claimant_record_scores_kernel(
         nc.vector.tensor_copy(v2_w[:], tab2_w[:].bitcast(U32).indirect(offs2_sb[:]))
 
         shift_rows = shift.rearrange("(i p) n -> p i n", p=P)
-        vec_sb = held([P, M_TILES], F32, "vec_sb", after="w1_bf0")
-        with nc.allow_non_contiguous_dma(reason="one value of vec for each row of a tile of claimants"):
-            nc.sync.dma_start(vec_sb[:], vec.rearrange("(i p) -> p i", p=P))
-
-        h_bf = [held([P, BANK, PACK], BF16, f"h_bf{u}") for u in range(HALVES)]
-        hq = [quantised(f"hq{u}", BANK) for u in range(HALVES)]
-        for c in range(CHUNKS):
-            u, first = divmod(c * CHUNK, BANK)
-            if c < per_half:
-                acc = h_banks[c]
-            else:
-                acc = bank([P, PACK, CHUNK])
-                h_pass(acc, 0, c)
-            h_pass(acc, 1, c)
-            th = work.tile([P, CHUNK, PACK], F32, name="th", bufs=CHUNKS)
-            nc.scalar.activation(th[:], acc[:].rearrange("p t n -> p n t"), ACT.Tanh)
-            nc.vector.tensor_tensor(h_bf[u][:, first : first + CHUNK, :], th[:], per_slot(gain_sb), ALU.mult)
-            if c == per_half:
-                quantise(hq[0], h_bf[0][:].rearrange("p n t -> p (n t)"))
 
         w3q = [quantised(f"w3q{u}", BANK) for u in range(S2 // BANK)]
 
@@ -272,10 +253,33 @@ def tile_list_claimant_record_scores_kernel(
         round_w3(0, 0)
         round_w3(0, 1)
         quantise(w3q[0], w3_bf[0][:])
+        vec_sb = held([P, M_TILES], F32, "vec_sb", after="g_bf1")
+        with nc.allow_non_contiguous_dma(reason="one value of vec for each row of a tile of claimants"):
+            nc.sync.dma_start(vec_sb[:], vec.rearrange("(i p) -> p i", p=P))
         shift_sb = [held([P, M_TILES // 2, NP], F32, "shift_sb0", after="tab_w1")]
         nc.sync.dma_start(shift_sb[0][:], shift_rows[:, : M_TILES // 2, :])
         shift_sb.append(held([P, M_TILES // 2, NP], F32, "shift_sb1", after="w1_raw0"))
         nc.sync.dma_start(shift_sb[1][:], shift_rows[:, M_TILES // 2 :, :])
+
+        h_bf = [held([P, BANK, PACK], BF16, f"h_bf{u}") for u in range(HALVES)]
+        hq = [quantised(f"hq{u}", BANK) for u in range(HALVES)]
+        for pair in range(CHUNKS // 2):
+            th = work.tile([P, 2 * CHUNK, PACK], F32, name="th", bufs=CHUNKS // 2)
+            for c in (2 * pair, 2 * pair + 1):
+                if c < per_half:
+                    acc = h_banks[c]
+                else:
+                    acc = bank([P, PACK, CHUNK])
+                    h_pass(acc, 0, c)
+                h_pass(acc, 1, c)
+                place = (c % 2) * CHUNK
+                nc.scalar.activation(th[:, place : place + CHUNK, :], acc[:].rearrange("p t n -> p n t"), ACT.Tanh)
+            u, first = divmod(2 * pair * CHUNK, BANK)
+            nc.vector.tensor_tensor(
+                h_bf[u][:, first : first + 2 * CHUNK, :], th[:], per_slot(gain_sb, 2 * CHUNK), ALU.mult
+            )
+            if 2 * pair == per_half:
+                quantise(hq[0], h_bf[0][:].rearrange("p n t -> p (n t)"))
 
         def product(weights, weight_scales, operand):
             acc = bank([P, BANK])
@@ -302,17 +306,16 @@ def tile_list_claimant_record_scores_kernel(
             nc.scalar.activation(a[:], e[:].indirect(pos1_sb[:]), ACT.Exp, bias=neg_top[:])
             return a
 
-        def scores_w3(i):
+        def scores_w3(i, u):
             w, first = divmod(i * P, BANK)
-            d2 = work.tile([P, S], F32, name="d2")
-            for u in range(HALVES):
-                acc = product(w3q[w][0][:, first : first + P], w3q[w][1][:, first : first + P], gq[u])
-                nc.scalar.copy(d2[:, half(u)], acc[:])
+            d2 = work.tile([P, BANK], F32, name=f"d2_{u}", bufs=2)
+            acc = product(w3q[w][0][:, first : first + P], w3q[w][1][:, first : first + P], gq[u])
+            nc.scalar.copy(d2[:], acc[:])
             return d2
 
         def scores_d(i, u, d, d2):
             acc = product(v2_w[:, rows(i)], v2_sc[:, rows(i)], gq[u])
-            nc.vector.tensor_tensor(d[:, half(u)], acc[:], d2[:, half(u)], ALU.max)
+            nc.vector.tensor_tensor(d[:, half(u)], acc[:], d2[:], ALU.max)
 
         def weigh(i, a):
             c = work.tile([P, NP], F32, name="c")
@@ -327,38 +330,38 @@ def tile_list_claimant_record_scores_kernel(
             nc.vector.tensor_tensor(o[:], d[:].indirect(pos2_sb[:]), c[:], ALU.mult)
             nc.sync.dma_start(out[rows(i), :], o[:])
 
-        def first_scores(i):
-            e = work.tile([P, S], F32, name="e", bufs=2)
-            tops = work.tile([P, HALVES], F32, name="tops")
-            scores_e(i, 0, e, tops[:, 0:1], None)
-            return e, tops
+        def score_tiles():
+            return work.tile([P, S], F32, name="e", bufs=2), work.tile([P, HALVES], F32, name="tops")
 
-        def last_scores(i, e, tops):
-            scores_e(i, 1, e, tops[:, 1:2], tops[:, 0:1])
-            return e, tops[:, 1:2]
-
-        begun = first_scores(0)
+        e, tops = score_tiles()
+        scores_e(0, 0, e, tops[:, 0:1], None)
         quantise(hq[1], h_bf[1][:].rearrange("p n t -> p (n t)"))
-        begun_next = first_scores(1)
-        weights = [weigh(0, look(*last_scores(0, *begun)))]
-        scored = last_scores(1, *begun_next)
-        second = [scores_w3(0), scores_w3(1)]
+        second = [[scores_w3(i, u) for u in range(HALVES)] for i in range(2)]
+        scores_e(0, 1, e, tops[:, 1:2], tops[:, 0:1])
+        weights = [weigh(0, look(e, tops[:, 1:2]))]
         round_w3(1, 0)
         round_w3(1, 1)
         loss = []
         for i in range(M_TILES):
+            next_e, next_w3 = i + 1 < M_TILES, i + 2 < M_TILES
             d = work.tile([P, S], F32, name="d")
-            for u in range(HALVES):
-                scores_d(i, u, d, second[i])
             loss.append(d)
+            if next_e:
+                e, tops = score_tiles()
+                scores_e(i + 1, 0, e, tops[:, 0:1], None)
+            scores_d(i, 0, d, second[i][0])
+            if next_w3:
+                second.append([scores_w3(i + 2, 0)])
+            if next_e:
+                scores_e(i + 1, 1, e, tops[:, 1:2], tops[:, 0:1])
+                a = look(e, tops[:, 1:2])
+            scores_d(i, 1, d, second[i][1])
+            if next_w3:
+                second[i + 2].append(scores_w3(i + 2, 1))
+            if next_e:
+                weights.append(weigh(i + 1, a))
             if i == 0:
                 quantise(w3q[1], w3_bf[1][:])
-            if i + 1 < M_TILES:
-                weights.append(weigh(i + 1, look(*scored)))
-            if i + 2 < M_TILES:
-                second.append(scores_w3(i + 2))
             if i > 0:
                 finish(i - 1, loss[i - 1], weights[i - 1])
-            if i + 2 < M_TILES:
-                scored = last_scores(i + 2, *first_scores(i + 2))
         finish(M_TILES - 1, loss[-1], weights[-1])

@@ -317,13 +317,19 @@ def tile_list_claimant_record_scores_kernel(
             acc = product(v2_w[:, rows(i)], v2_sc[:, rows(i)], gq[u])
             nc.vector.tensor_tensor(d[:, half(u)], acc[:], d2[:], ALU.max)
 
-        def weigh(i, a):
-            c = work.tile([P, NP], F32, name="c")
+        def shift_tile(i):
             part, place = divmod(i, M_TILES // 2)
+            return shift_sb[part][:, place, :]
+
+        def scale_look(i, a):
             scaled = work.tile([P, NP], F32, name="scaled")
             nc.scalar.activation(scaled[:], a[:], ACT.Copy, scale=vec_sb[:, i : i + 1])
-            nc.gpsimd.tensor_tensor(c[:], scaled[:], shift_sb[part][:, place, :], ALU.add)
-            return c
+            return scaled
+
+        def add_shift(i, scaled):
+            factor = work.tile([P, NP], F32, name="factor", bufs=1)
+            nc.gpsimd.tensor_tensor(factor[:], scaled[:], shift_tile(i), ALU.add)
+            return factor
 
         def finish(i, d, c):
             o = work.tile([P, NP], F32, name="o")
@@ -338,30 +344,38 @@ def tile_list_claimant_record_scores_kernel(
         quantise(hq[1], h_bf[1][:].rearrange("p n t -> p (n t)"))
         second = [[scores_w3(i, u) for u in range(HALVES)] for i in range(2)]
         scores_e(0, 1, e, tops[:, 1:2], tops[:, 0:1])
-        weights = [weigh(0, look(e, tops[:, 1:2]))]
+        scaled = [scale_look(0, look(e, tops[:, 1:2]))]
+        factor = add_shift(0, scaled[0])
         round_w3(1, 0)
         round_w3(1, 1)
+        last = M_TILES - 1
         loss = []
         for i in range(M_TILES):
-            next_e, next_w3 = i + 1 < M_TILES, i + 2 < M_TILES
             d = work.tile([P, S], F32, name="d")
             loss.append(d)
-            if next_e:
+            if i + 1 <= last:
                 e, tops = score_tiles()
                 scores_e(i + 1, 0, e, tops[:, 0:1], None)
             scores_d(i, 0, d, second[i][0])
-            if next_w3:
+            if i + 2 <= last:
                 second.append([scores_w3(i + 2, 0)])
-            if next_e:
+            if i + 1 <= last:
                 scores_e(i + 1, 1, e, tops[:, 1:2], tops[:, 0:1])
                 a = look(e, tops[:, 1:2])
             scores_d(i, 1, d, second[i][1])
-            if next_w3:
+            if i + 2 <= last:
                 second[i + 2].append(scores_w3(i + 2, 1))
-            if next_e:
-                weights.append(weigh(i + 1, a))
+            if i + 1 < last:
+                scaled.append(scale_look(i + 1, a))
             if i == 0:
                 quantise(w3q[1], w3_bf[1][:])
+            if i == last:
+                last_factor = work.tile([P, NP], F32, name="last_factor", bufs=1)
+                nc.vector.scalar_tensor_tensor(
+                    last_factor[:], a[:], vec_sb[:, last : last + 1], shift_tile(last), ALU.mult, ALU.add
+                )
             if i > 0:
-                finish(i - 1, loss[i - 1], weights[i - 1])
-        finish(M_TILES - 1, loss[-1], weights[-1])
+                finish(i - 1, loss[i - 1], factor)
+                if i < last:
+                    factor = add_shift(i, scaled[i])
+        finish(last, loss[last], last_factor)

from contextlib import ExitStack

import concourse.mybir as mybir

K, H, T, S, T3, S2, NP = 1024, 512, 4096, 1024, 2048, 1024, 512
FLOPS = 2 * (2 * K * H * S + 3 * H * S2 * S)

F32 = mybir.dt.float32
BF16 = mybir.dt.bfloat16
I32 = mybir.dt.int32
U32 = mybir.dt.uint32
U16 = mybir.dt.uint16
U8 = mybir.dt.uint8
FP8X4 = mybir.dt.float8_e4m3fn_x4
FP4X4 = mybir.dt.float4_e2m1fn_x4
ACT = mybir.ActivationFunctionType
ALU = mybir.AluOpType

P = 128
PACK = 4
K_PASS = P * PACK
PASSES = K // K_PASS
BANK = 512
HALVES = S // BANK
CHUNK = BANK // PACK
CHUNKS = S // CHUNK
M_TILES = S2 // P
QUADS = 4
LIST_ROWS = 16


def tile_list_claimant_record_scores_kernel(
    tc, tab_words, tab_scales, offs, tab2_words, tab2_scales, offs2, pos1, pos2,
    w1, gain, w2_words, w2_scales, b2, w3, vec, shift, out,
):
    nc = tc.nc
    with ExitStack() as ctx:
        keep = ctx.enter_context(tc.tile_pool(name="keep", bufs=1))
        work = ctx.enter_context(tc.tile_pool(name="work", bufs=3))
        psum = ctx.enter_context(tc.psum_pool(name="psum", bufs=8))

        def held(shape, dtype, name, after=None):
            return keep.tile(shape, dtype, name=name, tag=after or name, align_bytes=64)

        def bank(shape):
            return psum.tile(shape, F32, name="bank")

        offs_sb = keep.tile([P, S // LIST_ROWS], U16, name="offs_sb")
        offs2_sb = keep.tile([P, S2 // LIST_ROWS], U16, name="offs2_sb")
        pos1_sb = keep.tile([P, NP // LIST_ROWS], U16, name="pos1_sb")
        pos2_sb = keep.tile([P, NP // LIST_ROWS], U16, name="pos2_sb")

        tab_sc = held([P, T], U8, "tab_sc")
        w2_sc_raw = held([P, PASSES, H], U8, "w2_sc_raw")
        tab2_sc = held([P, T3], U8, "tab2_sc")
        v_sc = [held([P, S], U8, f"v_sc{a}") for a in range(PASSES)]
        v2_sc = held([P, S2], U8, "v2_sc")
        first_live = 32 - 4 * PASSES
        first_live2 = 32 - 4
        nc.gpsimd.memset(w2_sc_raw[:].bitcast(I32), 0)
        for q in range(QUADS):
            engine = nc.vector if q < QUADS // 2 else nc.gpsimd
            engine.memset(tab_sc[32 * q : 32 * q + first_live, :].bitcast(I32), 0)
        for plane in v_sc:
            nc.gpsimd.memset(plane[96:P, :].bitcast(I32), 0)
        for q in range(QUADS):
            nc.gpsimd.memset(tab2_sc[32 * q : 32 * q + first_live2, :].bitcast(I32), 0)
        nc.gpsimd.memset(v2_sc[96:P, :].bitcast(I32), 0)

        nc.sync.dma_start(offs_sb[:], offs)
        for q in range(QUADS):
            nc.sync.dma_start(
                tab_sc[32 * q + first_live : 32 * (q + 1), :].bitcast(I32),
                tab_scales[:, 4 * q : 4 * q + 4, :].bitcast(I32),
            )
        nc.sync.dma_start(offs2_sb[:], offs2)
        for q in range(QUADS):
            nc.sync.dma_start(
                tab2_sc[32 * q + first_live2 : 32 * (q + 1), :].bitcast(I32),
                tab2_scales[0, 4 * q : 4 * q + 4, :].bitcast(I32),
            )

        def table_words(words):
            return words.rearrange("p t i -> p (t i)").bitcast(I32)

        tab_w = [held([P, T], I32, f"tab_w{a}") for a in range(PASSES)]
        nc.sync.dma_start(tab_w[0][:], table_words(tab_words[0]))
        w2_raw = held([P, PASSES, 2 * H], U8, "w2_raw")
        nc.sync.dma_start(w2_raw[:].bitcast(I32), w2_words.rearrange("a p c -> p a c").bitcast(I32))
        for r in range(4):
            nc.sync.dma_start(
                w2_sc_raw[r : P : 32, :, :].bitcast(I32),
                w2_scales[:, r : 16 : 4, :].rearrange("a q c -> q a c").bitcast(I32),
            )
        b2_sb = held([P, PACK], F32, "b2_sb")
        gain_sb = held([P, PACK], F32, "gain_sb")
        nc.sync.dma_start(b2_sb[:], b2.rearrange("(p t) -> p t", t=PACK))
        nc.sync.dma_start(tab_w[1][:], table_words(tab_words[1]))

        def load_w1(a, after):
            raw = held([P, PACK, H], F32, f"w1_raw{a}", after=after)
            nc.sync.dma_start(raw[:], w1[a * K_PASS : (a + 1) * K_PASS, :].rearrange("(p j) c -> p j c", j=PACK))
            return raw

        w1_raw = [load_w1(0, None)]
        nc.sync.dma_start(gain_sb[:], gain.rearrange("(p t) -> p t", t=PACK))
        nc.sync.dma_start(pos1_sb[:], pos1)
        nc.sync.dma_start(pos2_sb[:], pos2)

        live = 32 * (QUADS - 1) + 4

        def to_row_0(plane, gathered, first):
            nc.scalar.dma_start(plane[0:live, :].bitcast(I32), gathered[first : first + live, :].bitcast(I32))

        v_sc_both = held([P, S], U8, "v_sc_both")
        nc.vector.tensor_copy(v_sc_both[:], tab_sc[:].indirect(offs_sb[:]))
        for a in range(PASSES):
            to_row_0(v_sc[a], v_sc_both, first_live + 4 * a)
        v2_sc_low = held([P, S2], U8, "v2_sc_low")
        nc.vector.tensor_copy(v2_sc_low[:], tab2_sc[:].indirect(offs2_sb[:]))
        to_row_0(v2_sc, v2_sc_low, first_live2)

        cols = BANK // LIST_ROWS
        v_w = [[held([P, BANK], U32, f"v_w{a}{u}") for u in range(HALVES)] for a in range(PASSES)]

        def gather_records(a):
            for u in range(HALVES):
                nc.vector.tensor_copy(
                    v_w[a][u][:], tab_w[a][:].bitcast(U32).indirect(offs_sb[:, u * cols : (u + 1) * cols])
                )

        def records(a, c):
            u, first = divmod(c * CHUNK, BANK)
            return v_w[a][u][:, first : first + CHUNK].bitcast(FP8X4)

        w2_w = held([P, PASSES, 2 * H], U8, "w2_w")
        w2_sc = held([P, PASSES, H], U8, "w2_sc")
        nc.vector.tensor_copy(
            w2_w[:].bitcast(U16).rearrange("p a (t q) -> p a t q", t=PACK),
            w2_raw[:].bitcast(U16).rearrange("p a (q t) -> p a t q", t=PACK),
        )
        nc.vector.tensor_copy(
            w2_sc[:].rearrange("p a (t q) -> p a t q", t=PACK),
            w2_sc_raw[:].rearrange("p a (q t) -> p a t q", t=PACK),
        )

        gather_records(0)
        w1_raw.append(load_w1(1, "tab_w0"))
        gather_records(1)

        def load_w3(u, after):
            raw = held([P, PACK, BANK], F32, f"w3_raw{u}", after=after)
            nc.sync.dma_start(raw[:], w3[:, u * BANK : (u + 1) * BANK].rearrange("(p j) c -> p j c", j=PACK))
            return raw

        w3_raw = [load_w3(0, "tab_w1")]

        g_banks = [bank([P, PACK, CHUNK]) for c in range(CHUNKS)]

        def g_pass(a, c):
            for t in range(PACK):
                nc.tensor.matmul_mx(
                    out=g_banks[c][:, t, :],
                    lhsT=w2_w[:, a, 2 * P * t : 2 * P * (t + 1)].bitcast(FP4X4),
                    lhsT_scale=w2_sc[:, a, P * t : P * (t + 1)],
                    rhs=records(a, c),
                    rhs_scale=v_sc[a][:, c * CHUNK : (c + 1) * CHUNK],
                    start=(a == 0 and t == 0),
                    stop=(a == PASSES - 1 and t == PACK - 1),
                )

        for c in range(CHUNKS):
            g_pass(0, c)
        for c in range(CHUNKS):
            g_pass(1, c)

        def quantised(name, width):
            return held([P, width], U32, f"{name}_w"), held([P, width], U8, f"{name}_sc")

        def quantise(dst, src):
            nc.vector.quantize_mx(out=dst[0][:].bitcast(FP8X4), scales=dst[1][:], in_=src)

        def per_slot(values, columns):
            return values[:].unsqueeze(1).to_broadcast([P, columns, PACK])

        w1q = [quantised(f"w1q{a}", H) for a in range(PASSES)]

        def quantise_w1(a):
            w1_bf = held([P, H * PACK], BF16, f"w1_bf{a}")
            nc.scalar.activation(
                w1_bf[:].rearrange("p (t m j) -> p m t j", t=PACK, j=PACK),
                w1_raw[a][:].rearrange("p j (m t) -> p m t j", t=PACK),
                ACT.Copy,
            )
            quantise(w1q[a], w1_bf[:])

        per_half = CHUNKS // HALVES
        g_bf = [held([P, BANK, PACK], BF16, f"g_bf{u}") for u in range(HALVES)]
        gq = [quantised(f"gq{u}", BANK) for u in range(HALVES)]
        for c in range(CHUNKS):
            u, first = divmod(c * CHUNK, BANK)
            nc.vector.tensor_tensor(
                g_bf[u][:, first : first + CHUNK, :],
                g_banks[c][:].rearrange("p t n -> p n t"),
                per_slot(b2_sb, CHUNK),
                ALU.add,
            )
            if c == per_half - 1:
                quantise_w1(0)
            if c == per_half:
                quantise(gq[0], g_bf[0][:].rearrange("p n t -> p (n t)"))

        tab2_w = held([P, T3], I32, "tab2_w", after="w1_raw0")
        nc.sync.dma_start(tab2_w[:], table_words(tab2_words[0]))

        def h_pass(acc, a, c):
            for t in range(PACK):
                nc.tensor.matmul_mx(
                    out=acc[:, t, :],
                    lhsT=w1q[a][0][:, P * t : P * (t + 1)].bitcast(FP8X4),
                    lhsT_scale=w1q[a][1][:, P * t : P * (t + 1)],
                    rhs=records(a, c),
                    rhs_scale=v_sc[a][:, c * CHUNK : (c + 1) * CHUNK],
                    start=(a == 0 and t == 0),
                    stop=(a == PASSES - 1 and t == PACK - 1),
                )

        h_banks = [bank([P, PACK, CHUNK]) for c in range(per_half)]
        for c in range(per_half):
            h_pass(h_banks[c], 0, c)

        quantise_w1(1)
        w3_raw.append(load_w3(1, "tab_w0"))
        quantise(gq[1], g_bf[1][:].rearrange("p n t -> p (n t)"))

        v2_w = held([P, S2], U32, "v2_w", after="w1_bf1")
        nc.vector.tensor_copy(v2_w[:], tab2_w[:].bitcast(U32).indirect(offs2_sb[:]))

        shift_rows = shift.rearrange("(i p) n -> p i n", p=P)

        w3q = [quantised(f"w3q{u}", BANK) for u in range(S2 // BANK)]

        w3_bf = [held([P, BANK * PACK], BF16, f"w3_bf{u}") for u in range(S2 // BANK)]
        piece = BANK // 2

        def round_w3(u, v):
            nc.scalar.activation(
                w3_bf[u][:, v * piece * PACK : (v + 1) * piece * PACK].rearrange("p (c i j) -> p c j i", i=4, j=PACK),
                w3_raw[u][:, :, v * piece : (v + 1) * piece].rearrange("p j (c i) -> p c j i", i=4),
                ACT.Copy,
            )

        round_w3(0, 0)
        round_w3(0, 1)
        quantise(w3q[0], w3_bf[0][:])
        vec_sb = held([P, M_TILES], F32, "vec_sb", after="g_bf1")
        with nc.allow_non_contiguous_dma(reason="one value of vec for each row of a tile of claimants"):
            nc.sync.dma_start(vec_sb[:], vec.rearrange("(i p) -> p i", p=P))
        shift_sb = [held([P, M_TILES // 2, NP], F32, "shift_sb0", after="tab_w1")]
        nc.sync.dma_start(shift_sb[0][:], shift_rows[:, : M_TILES // 2, :])
        shift_sb.append(held([P, M_TILES // 2, NP], F32, "shift_sb1", after="w1_raw0"))
        nc.sync.dma_start(shift_sb[1][:], shift_rows[:, M_TILES // 2 :, :])

        h_bf = [held([P, BANK, PACK], BF16, f"h_bf{u}") for u in range(HALVES)]
        hq = [quantised(f"hq{u}", BANK) for u in range(HALVES)]
        for pair in range(CHUNKS // 2):
            th = work.tile([P, 2 * CHUNK, PACK], F32, name="th", bufs=CHUNKS // 2)
            for c in (2 * pair, 2 * pair + 1):
                if c < per_half:
                    acc = h_banks[c]
                else:
                    acc = bank([P, PACK, CHUNK])
                    h_pass(acc, 0, c)
                h_pass(acc, 1, c)
                place = (c % 2) * CHUNK
                nc.scalar.activation(th[:, place : place + CHUNK, :], acc[:].rearrange("p t n -> p n t"), ACT.Tanh)
            u, first = divmod(2 * pair * CHUNK, BANK)
            nc.vector.tensor_tensor(
                h_bf[u][:, first : first + 2 * CHUNK, :], th[:], per_slot(gain_sb, 2 * CHUNK), ALU.mult
            )
            if 2 * pair == per_half:
                quantise(hq[0], h_bf[0][:].rearrange("p n t -> p (n t)"))

        def product(weights, weight_scales, operand):
            acc = bank([P, BANK])
            nc.tensor.matmul_mx(
                out=acc[:], lhsT=weights.bitcast(FP8X4), lhsT_scale=weight_scales,
                rhs=operand[0][:].bitcast(FP8X4), rhs_scale=operand[1][:], start=True, stop=True,
            )
            return acc

        def rows(i):
            return slice(i * P, (i + 1) * P)

        def half(u):
            return slice(u * BANK, (u + 1) * BANK)

        def scores_e(i, u, e, top, top_so_far):
            acc = product(v2_w[:, rows(i)], v2_sc[:, rows(i)], hq[u])
            nc.vector.tensor_scalar(e[:, half(u)], acc[:], 1.0, top_so_far, ALU.mult, ALU.max, accum_out=top)

        def look(e, top):
            neg_top = work.tile([P, 1], F32, name="neg_top")
            nc.scalar.activation(neg_top[:], top, ACT.Copy, scale=-1.0)
            a = work.tile([P, NP], F32, name="a")
            nc.scalar.activation(a[:], e[:].indirect(pos1_sb[:]), ACT.Exp, bias=neg_top[:])
            return a

        def scores_w3(i, u):
            w, first = divmod(i * P, BANK)
            d2 = work.tile([P, BANK], F32, name=f"d2_{u}", bufs=2)
            acc = product(w3q[w][0][:, first : first + P], w3q[w][1][:, first : first + P], gq[u])
            nc.scalar.copy(d2[:], acc[:])
            return d2

        def scores_d(i, u, d, d2):
            acc = product(v2_w[:, rows(i)], v2_sc[:, rows(i)], gq[u])
            nc.vector.tensor_tensor(d[:, half(u)], acc[:], d2[:], ALU.max)

        def shift_tile(i):
            part, place = divmod(i, M_TILES // 2)
            return shift_sb[part][:, place, :]

        def scale_look(i, a):
            scaled = work.tile([P, NP], F32, name="scaled")
            nc.scalar.activation(scaled[:], a[:], ACT.Copy, scale=vec_sb[:, i : i + 1])
            return scaled

        def add_shift(i, scaled):
            factor = work.tile([P, NP], F32, name="factor", bufs=1)
            nc.gpsimd.tensor_tensor(factor[:], scaled[:], shift_tile(i), ALU.add)
            return factor

        def finish(i, d, c):
            o = work.tile([P, NP], F32, name="o")
            nc.vector.tensor_tensor(o[:], d[:].indirect(pos2_sb[:]), c[:], ALU.mult)
            nc.sync.dma_start(out[rows(i), :], o[:])

        def score_tiles():
            return work.tile([P, S], F32, name="e", bufs=2), work.tile([P, HALVES], F32, name="tops")

        e, tops = score_tiles()
        scores_e(0, 0, e, tops[:, 0:1], None)
        quantise(hq[1], h_bf[1][:].rearrange("p n t -> p (n t)"))
        second = [[scores_w3(i, u) for u in range(HALVES)] for i in range(2)]
        scores_e(0, 1, e, tops[:, 1:2], tops[:, 0:1])
        scaled = [scale_look(0, look(e, tops[:, 1:2]))]
        factor = add_shift(0, scaled[0])
        round_w3(1, 0)
        round_w3(1, 1)
        last = M_TILES - 1
        loss = []
        for i in range(M_TILES):
            d = work.tile([P, S], F32, name="d")
            loss.append(d)
            if i + 1 <= last:
                e, tops = score_tiles()
                scores_e(i + 1, 0, e, tops[:, 0:1], None)
            scores_d(i, 0, d, second[i][0])
            if i + 2 <= last:
                second.append([scores_w3(i + 2, 0)])
            if i + 1 <= last:
                scores_e(i + 1, 1, e, tops[:, 1:2], tops[:, 0:1])
                a = look(e, tops[:, 1:2])
            scores_d(i, 1, d, second[i][1])
            if i + 2 <= last:
                second[i + 2].append(scores_w3(i + 2, 1))
            if i + 1 < last:
                scaled.append(scale_look(i + 1, a))
            if i == 0:
                quantise(w3q[1], w3_bf[1][:])
            if i == last:
                last_factor = work.tile([P, NP], F32, name="last_factor", bufs=1)
                nc.vector.scalar_tensor_tensor(
                    last_factor[:], a[:], vec_sb[:, last : last + 1], shift_tile(last), ALU.mult, ALU.add
                )
            if i > 0:
                finish(i - 1, loss[i - 1], factor)
                if i < last:
                    factor = add_shift(i, scaled[i])
        finish(last, loss[last], last_factor)
